import numpy as np
import ml_dtypes


def mxq(x, axis, fmt="e4m3"):
    dtype, down = {"e4m3": (ml_dtypes.float8_e4m3fn, 7), "e5m2": (ml_dtypes.float8_e5m2, 14)}[fmt]
    v = np.moveaxis(np.asarray(x, np.float32).astype(ml_dtypes.bfloat16).astype(np.float64), axis, -1)
    blocks = v.reshape(v.shape[:-1] + (-1, 32))
    amax = np.abs(blocks).max(-1, keepdims=True)
    byte = np.maximum(np.where(amax > 0, np.frexp(amax)[1] - 1 + 127, 0) - down, 1)
    scale = np.exp2(byte - 127.0)
    codes = (blocks / scale).astype(np.float32).astype(dtype).astype(np.float64)
    return np.moveaxis((codes * scale).reshape(v.shape), -1, axis)


WIDE = False


def mx_kscale(k):
    if not WIDE:
        return np.ones(k)
    levels = np.array([10, -10, 5, -5, 0])
    if k % 512:
        return np.exp2(np.random.permutation(np.resize(levels, k // 32))).repeat(32)
    a = np.empty((k // 512, 16))
    for p in range(k // 512):
        a[p, :8] = np.random.permutation(np.resize(levels, 8))
        for g in range(8):
            far = levels[np.abs(levels - a[p, g]) >= 10]
            a[p, g + 8] = far[np.random.randint(len(far))]
    return np.exp2(a.ravel()).repeat(32)


def f64(x):
    return np.asarray(x).astype(np.float64)


def striped(idx):
    return np.tile(idx.reshape(-1, 16).T, (8, 1)).astype(np.uint16)


def unstriped(offs):
    return offs[:16].T.reshape(-1).astype(np.int64)


E2M1 = np.array([0.0, 0.5, 1.0, 1.5, 2.0, 3.0, 4.0, 6.0, -0.0, -0.5, -1.0, -1.5, -2.0, -3.0, -4.0, -6.0])


def pack_weight(w, fmt):
    k, n = w.shape
    w = f64(np.asarray(w, np.float32).astype(ml_dtypes.bfloat16)).reshape(k // 32, 32, n)
    amax = np.abs(w).max(1)
    if fmt == "e4m3":
        byte = np.frexp(amax)[1] - 1 + 127 - 7
    else:
        mant, ex = np.frexp(amax / 6.0)
        byte = np.where(mant > 0.5, ex, ex - 1) + 127
    byte = np.clip(np.where(amax > 0, byte, 1), 1, 254)
    scaled = (w * np.exp2(127.0 - byte)[:, None, :]).reshape(k, n).astype(np.float32)
    by_word = np.ascontiguousarray(scaled.reshape(k // 512, 128, 4, n).transpose(0, 1, 3, 2))
    if fmt == "e4m3":
        words = by_word.astype(ml_dtypes.float8_e4m3fn).view(np.uint8)
    else:
        c = by_word.astype(ml_dtypes.float4_e2m1fn).view(np.uint8) & 0xF
        words = (c[..., 0::2] | (c[..., 1::2] << 4)).reshape(k // 512, 128, 2 * n)
    return np.ascontiguousarray(words), np.ascontiguousarray(byte.astype(np.uint8).reshape(k // 512, 16, n))


def unpack_weight(words, scales, fmt):
    g, _, n = scales.shape
    words = np.ascontiguousarray(words).reshape(g, 128, n, -1)
    if fmt == "e4m3":
        vals = words.view(ml_dtypes.float8_e4m3fn).astype(np.float64)
    else:
        nib = np.empty((g, 128, n, 4), np.uint8)
        nib[..., 0::2] = words & 0xF
        nib[..., 1::2] = words >> 4
        vals = E2M1[nib]
    vals = vals * np.repeat(np.exp2(scales.astype(np.float64) - 127.0), 8, axis=1)[..., None]
    return vals.transpose(0, 1, 3, 2).reshape(g * 512, n)


def gelu(v):
    return 0.5 * v * (1.0 + np.tanh(np.sqrt(2.0 / np.pi) * (v + 0.044715 * v**3)))


def striped8(idx):
    return np.concatenate([v.reshape(-1, 16).T for v in idx]).astype(np.uint16)


def unstriped8(offs):
    return np.stack([offs[16 * g:16 * g + 16].T.reshape(-1) for g in range(8)]).astype(np.int64)


def heads(h, wgt, idx8):
    r = np.arange(h.shape[0])
    return wgt[r // 4 % 128] * h[r[:, None], idx8[r % 512 // 64]]


K, H, N, T, S, P = 1024, 512, 768, 4096, 1024, 512

def setup_inputs():
    n = np.random.standard_normal
    s = mx_kscale(K)[:, None]
    u = mx_kscale(H)[:, None]
    tab_words, tab_scales = pack_weight(n((K, T)) * s, "e4m3")
    we_words, we_scales = pack_weight(0.75 * n((K, H)) / np.sqrt(K) / s, "e2m1")
    wy_words, wy_scales = pack_weight(n((H, N)) / np.sqrt(H) / u, "e4m3")
    return {
        "tab_words": tab_words, "tab_scales": tab_scales,
        "offs": striped(np.random.permutation(T)[:S]),
        "offs2": striped8(np.stack([np.random.permutation(S)[:P] for _ in range(8)])),
        "offs3": striped8(np.stack([np.random.permutation(S)[:P] for _ in range(8)])),
        "wp": (n((K, H)) / np.sqrt(K) / s * u.T).astype(np.float32),
        "bp": (0.5 * n(H) * u[:, 0]).astype(np.float32),
        "wb": (0.7 * n((K, H)) / np.sqrt(K) / s * u.T).astype(np.float32),
        "we_words": we_words, "we_scales": we_scales,
        "wga": np.repeat(np.random.uniform(0.5, 2.0, (8, P)), 16, axis=0).astype(np.float32),
        "wgb": np.repeat(np.random.uniform(0.5, 2.0, (8, P)), 16, axis=0).astype(np.float32),
        "wy_words": wy_words, "wy_scales": wy_scales,
        "by": (0.5 * n(N)).astype(np.float32),
    }

def reference(tab_words, tab_scales, offs, offs2, offs3, wp, bp, wb, we_words, we_scales, wga, wgb, wy_words, wy_scales, by):
    v = unpack_weight(tab_words, tab_scales, "e4m3")[:, unstriped(offs)]
    we = unpack_weight(we_words, we_scales, "e2m1")
    wy = unpack_weight(wy_words, wy_scales, "e4m3")
    hp = (mxq(f64(wp), 0, "e4m3").T @ v) + f64(bp)[:, None]
    eb = np.exp(we.T @ v)
    hb = (mxq(f64(wb), 0, "e4m3").T @ v) * eb
    xa = heads(hp, f64(wga), unstriped8(offs2))
    xb = heads(hb, f64(wgb), unstriped8(offs3))
    z = np.maximum(xa, xb)
    y = (wy.T @ mxq(z, 0, "e4m3")) + f64(by)[:, None]
    return np.tanh(y)

@@ -1,0 +1,204 @@
+from contextlib import ExitStack
+
+import concourse.mybir as mybir
+
+K, H, N, T, S, M = 1024, 512, 768, 4096, 1024, 512
+FLOPS = 2 * (3 * K * H * S + H * N * M)
+
+F32 = mybir.dt.float32
+BF16 = mybir.dt.bfloat16
+I32 = mybir.dt.int32
+U32 = mybir.dt.uint32
+U16 = mybir.dt.uint16
+U8 = mybir.dt.uint8
+FP8X4 = mybir.dt.float8_e4m3fn_x4
+FP4X4 = mybir.dt.float4_e2m1fn_x4
+ACT = mybir.ActivationFunctionType
+ALU = mybir.AluOpType
+
+P = 128
+PACK = 4
+PASSES = K // (P * PACK)
+BANK = 512
+HALVES = S // BANK
+N_TILES = N // P
+QUADS = 4
+KIB = 1024
+PIECES = ((0, 384), (384, 128))
+STORE_TILES = 2
+
+
+def tile_list_phage_host_lysis_kernel(tc, tab_words, tab_scales, offs, offs2, offs3, wp, bp, wb,
+                                                we_words, we_scales, wga, wgb, wy_words, wy_scales, by, out):
+    nc = tc.nc
+    with ExitStack() as ctx:
+        lists = ctx.enter_context(tc.tile_pool(name="lists", bufs=1))
+        keep = ctx.enter_context(tc.tile_pool(name="keep", bufs=1))
+        shared = ctx.enter_context(tc.tile_pool(name="shared", bufs=1))
+        psum = ctx.enter_context(tc.psum_pool(name="psum", bufs=8))
+
+        def placed(shape, dtype, name, kib):
+            return shared.tile(shape, dtype, name=name, offset=kib * KIB, align_bytes=64)
+
+        def kept(shape, dtype, name):
+            return keep.tile(shape, dtype, name=name, align_bytes=64)
+
+        offs_sb = lists.tile([P, S // 16], U16, name="offs_sb")
+        offs2_sb = lists.tile([P, M // 16], U16, name="offs2_sb")
+        offs3_sb = lists.tile([P, M // 16], U16, name="offs3_sb")
+        nc.sync.dma_start(offs_sb[:], offs)
+
+        scale_rows = placed([P, T], U8, "scale_rows", 0)
+        nc.sync.dma_start(scale_rows[0:32, :].bitcast(I32), tab_scales.rearrange("a q t -> (a q) t").bitcast(I32))
+        nc.vector.memset(scale_rows[32:64, :].bitcast(I32), 0)
+        nc.vector.memset(scale_rows[64:128, :].bitcast(I32), 0)
+        nc.sync.dma_start(offs3_sb[:], offs3)
+        nc.sync.dma_start(offs2_sb[:], offs2)
+
+        we_raw = kept([P, PASSES, 2 * H], U8, "we_raw")
+        nc.sync.dma_start(we_raw[:].bitcast(I32), we_words.rearrange("a p c -> p a c").bitcast(I32))
+        table = [placed([P, T], U32, "table%d" % a, 8 + 19 * a) for a in range(PASSES)]
+        for a in range(PASSES):
+            nc.sync.dma_start(table[a][:].bitcast(I32), tab_words[a].rearrange("p t i -> p (t i)").bitcast(I32))
+
+        we_raw_scales = kept([P, PASSES, H], U8, "we_raw_scales")
+        nc.gpsimd.memset(we_raw_scales[:].bitcast(I32), 0)
+        for q in range(QUADS):
+            nc.gpsimd.dma_start(we_raw_scales[32 * q:32 * q + 4].bitcast(I32),
+                                we_scales[:, 4 * q:4 * q + 4, :].rearrange("a r c -> r a c").bitcast(I32))
+
+        picked_rows = kept([P, S], U8, "picked_rows")
+        nc.vector.tensor_copy(picked_rows[:], scale_rows[:].indirect(offs_sb[:]))
+        v_scales = [kept([P, S], U8, "v_scales%d" % a) for a in range(PASSES)]
+        for a in range(PASSES):
+            nc.vector.memset(v_scales[a][:].bitcast(I32), 0)
+        for q in range(QUADS):
+            for a in range(PASSES):
+                queue = nc.scalar if q < QUADS - 1 else nc.gpsimd
+                row = 16 * a + 4 * q
+                queue.dma_start(v_scales[a][32 * q:32 * q + 4, :].bitcast(I32), picked_rows[row:row + 4, :].bitcast(I32))
+
+        we_codes = kept([P, PASSES, 2 * H], U8, "we_codes")
+        nc.vector.tensor_copy(we_codes[:].rearrange("p a (t m b) -> p a m t b", t=PACK, b=2),
+                              we_raw[:].rearrange("p a (m t b) -> p a m t b", t=PACK, b=2))
+        v_codes = [kept([P, S], U32, "v_codes%d" % a) for a in range(PASSES)]
+        for a in range(PASSES):
+            nc.vector.tensor_copy(v_codes[a][:], table[a][:].indirect(offs_sb[:]))
+
+        we_planes = placed([P, PASSES, H], U8, "we_planes", 18)
+        nc.vector.tensor_copy(we_planes[:].rearrange("p a (t m) -> p a m t", t=PACK),
+                              we_raw_scales[:].rearrange("p a (m t) -> p a m t", t=PACK))
+
+        def load_weight(w, a, name, kib):
+            raw = placed([P, PACK * H], F32, name, kib)
+            nc.sync.dma_start(raw[:], w[512 * a:512 * (a + 1), :].rearrange("(p j) c -> p (j c)", j=PACK))
+            return raw
+
+        wb_raw = [load_weight(wb, 0, "wb_raw0", 0), load_weight(wb, 1, "wb_raw1", 8)]
+        wgb_sb = placed([P, M], F32, "wgb_sb", 16)
+        nc.sync.dma_start(wgb_sb[:], wgb)
+        wp_raw = [load_weight(wp, 0, "wp_raw0", 19), load_weight(wp, 1, "wp_raw1", 27)]
+        bp_sb = placed([P, PACK], F32, "bp_sb", 35)
+        nc.sync.dma_start(bp_sb[:], bp.rearrange("(p t) -> p t", t=PACK))
+        wga_sb = placed([P, M], F32, "wga_sb", 36)
+        nc.sync.dma_start(wga_sb[:], wga)
+        wy_codes = placed([P, N], U32, "wy_codes", 38)
+        nc.sync.dma_start(wy_codes[:].bitcast(I32), wy_words[0].rearrange("p c i -> p (c i)").bitcast(I32))
+        by_sb = placed([P, N_TILES], F32, "by_sb", 41)
+        with nc.allow_non_contiguous_dma(reason="one bias value for each output row"):
+            nc.sync.dma_start(by_sb[:], by.rearrange("(j p) -> p j", p=P))
+        wy_plane = placed([P, N], U8, "wy_plane", 42)
+        nc.gpsimd.memset(wy_plane[:].bitcast(I32), 0)
+        for q in range(QUADS):
+            nc.gpsimd.dma_start(wy_plane[32 * q:32 * q + 4, :].bitcast(I32), wy_scales[0, 4 * q:4 * q + 4, :].bitcast(I32))
+
+        def first_stage(codes, planes, dtype, t, h):
+            acc = psum.tile([P, BANK], F32, name="acc")
+            cols = slice(BANK * h, BANK * (h + 1))
+            for a in range(PASSES):
+                nc.tensor.matmul_mx(acc[:], lhsT=codes(a, t).bitcast(dtype), lhsT_scale=planes(a, t),
+                                    rhs=v_codes[a][:, cols].bitcast(FP8X4), rhs_scale=v_scales[a][:, cols],
+                                    start=(a == 0), stop=(a == PASSES - 1))
+            return acc, cols
+
+        def round_weight(copy, raw, rounded):
+            copy(rounded[:].rearrange("p (t m j) -> p m j t", t=PACK, j=PACK),
+                 raw[:].rearrange("p (j m t) -> p m j t", t=PACK, j=PACK))
+
+        def quantise_weight(rounded, name):
+            codes = kept([P, H], U32, name + "_codes")
+            plane = kept([P, H], U8, name + "_plane")
+            for t in range(PACK):
+                nc.vector.quantize_mx(codes[:, P * t:P * (t + 1)].bitcast(FP8X4), plane[:, P * t:P * (t + 1)],
+                                      rounded[:, PACK * P * t:PACK * P * (t + 1)])
+            return codes, plane
+
+        eb = [kept([P, S], F32, "eb%d" % t) for t in range(PACK)]
+        for t in range(PACK):
+            for h in range(HALVES):
+                acc, cols = first_stage(lambda a, t: we_codes[:, a, 2 * P * t:2 * P * (t + 1)],
+                                        lambda a, t: we_planes[:, a, P * t:P * (t + 1)], FP4X4, t, h)
+                nc.scalar.activation(eb[t][:, cols], acc[:], ACT.Exp)
+
+        wb_mx = []
+        for a in range(PASSES):
+            rounded = kept([P, PACK * H], BF16, "wb_rounded%d" % a)
+            round_weight(nc.vector.tensor_copy, wb_raw[a], rounded)
+            wb_mx.append(quantise_weight(rounded, "wb%d" % a))
+        hb = [kept([P, S], F32, "hb%d" % t) for t in range(PACK)]
+        for t in range(PACK):
+            for h in range(HALVES):
+                acc, cols = first_stage(lambda a, t: wb_mx[a][0][:, P * t:P * (t + 1)],
+                                        lambda a, t: wb_mx[a][1][:, P * t:P * (t + 1)], FP8X4, t, h)
+                nc.vector.tensor_tensor(hb[t][:, cols], acc[:], eb[t][:, cols], ALU.mult)
+
+        wp_mx = []
+        for a in range(PASSES):
+            rounded = placed([P, PACK * H], BF16, "wp_rounded%d" % a, 43 + 4 * a)
+            round_weight(nc.scalar.copy, wp_raw[a], rounded)
+            wp_mx.append(quantise_weight(rounded, "wp%d" % a))
+        hp = [kept([P, S], F32, "hp%d" % t) for t in range(PACK)]
+        for t in range(PACK):
+            for h in range(HALVES):
+                acc, cols = first_stage(lambda a, t: wp_mx[a][0][:, P * t:P * (t + 1)],
+                                        lambda a, t: wp_mx[a][1][:, P * t:P * (t + 1)], FP8X4, t, h)
+                nc.scalar.activation(hp[t][:, cols], acc[:], ACT.Identity, bias=bp_sb[:, t:t + 1])
+
+        def pick(picked, h_tiles, offsets, weights, m0, width):
+            for t in range(PACK):
+                nc.vector.tensor_tensor(picked[:, t, :], h_tiles[t][:].indirect(offsets[:, m0 // 16:(m0 + width) // 16]),
+                                        weights[:, m0:m0 + width], ALU.mult)
+
+        xb = []
+        for piece, (m0, width) in enumerate(PIECES):
+            if piece == 0:
+                picked = placed([P, PACK, width], F32, "xb0", 47)
+            else:
+                picked = kept([P, PACK, width], F32, "xb%d" % piece)
+            pick(picked, hb, offs3_sb, wgb_sb, m0, width)
+            xb.append(picked)
+
+        out_rows = out.rearrange("(j p) m -> p j m", p=P)
+        for piece, (m0, width) in enumerate(PIECES):
+            xa = placed([P, PACK, width], F32, "xa%d" % piece, 53)
+            pick(xa, hp, offs2_sb, wga_sb, m0, width)
+            z = kept([P, PACK * width], BF16, "z%d" % piece)
+            nc.vector.tensor_tensor(z[:].rearrange("p (c i t) -> p c t i", i=4, t=PACK),
+                                    xa[:].rearrange("p t (c i) -> p c t i", i=4),
+                                    xb[piece][:].rearrange("p t (c i) -> p c t i", i=4), ALU.max)
+            z_codes = kept([P, width], U32, "z_codes%d" % piece)
+            z_plane = kept([P, width], U8, "z_plane%d" % piece)
+            nc.vector.quantize_mx(z_codes[:].bitcast(FP8X4), z_plane[:], z[:])
+            scores = kept([P, N_TILES, width], F32, "scores%d" % piece)
+            for j in range(N_TILES):
+                acc = psum.tile([P, BANK], F32, name="acc")
+                for c0 in range(0, width, 256):
+                    cols = slice(c0, min(c0 + 256, width))
+                    nc.tensor.matmul_mx(acc[:, cols], lhsT=wy_codes[:, P * j:P * (j + 1)].bitcast(FP8X4),
+                                        lhsT_scale=wy_plane[:, P * j:P * (j + 1)],
+                                        rhs=z_codes[:, cols].bitcast(FP8X4), rhs_scale=z_plane[:, cols],
+                                        start=True, stop=True)
+                nc.scalar.activation(scores[:, j, :], acc[:, 0:width], ACT.Tanh, bias=by_sb[:, j:j + 1])
+                if j % STORE_TILES == STORE_TILES - 1:
+                    rows = slice(j + 1 - STORE_TILES, j + 1)
+                    nc.sync.dma_start(out_rows[:, rows, m0:m0 + width], scores[:, rows, :])

@@ -35,7 +35,7 @@ def tile_list_phage_host_lysis_kernel(tc, tab_words, tab_scales, offs, offs2, of
         lists = ctx.enter_context(tc.tile_pool(name="lists", bufs=1))
         keep = ctx.enter_context(tc.tile_pool(name="keep", bufs=1))
         shared = ctx.enter_context(tc.tile_pool(name="shared", bufs=1))
-        psum = ctx.enter_context(tc.psum_pool(name="psum", bufs=8))
+        psum = ctx.enter_context(tc.psum_pool(name="psum", bufs=4))
 
         def placed(shape, dtype, name, kib):
             return shared.tile(shape, dtype, name=name, offset=kib * KIB, align_bytes=64)
@@ -52,31 +52,32 @@ def tile_list_phage_host_lysis_kernel(tc, tab_words, tab_scales, offs, offs2, of
         nc.sync.dma_start(scale_rows[0:32, :].bitcast(I32), tab_scales.rearrange("a q t -> (a q) t").bitcast(I32))
         nc.vector.memset(scale_rows[32:64, :].bitcast(I32), 0)
         nc.vector.memset(scale_rows[64:128, :].bitcast(I32), 0)
+        we_scale_rows = kept([P, H], U8, "we_scale_rows")
+        nc.sync.dma_start(we_scale_rows[0:32, :].bitcast(I32), we_scales.rearrange("a q c -> (a q) c").bitcast(I32))
+        nc.vector.memset(we_scale_rows[32:64, :].bitcast(I32), 0)
+        nc.vector.memset(we_scale_rows[64:128, :].bitcast(I32), 0)
         nc.sync.dma_start(offs3_sb[:], offs3)
         nc.sync.dma_start(offs2_sb[:], offs2)
 
         we_raw = kept([P, PASSES, 2 * H], U8, "we_raw")
         nc.sync.dma_start(we_raw[:].bitcast(I32), we_words.rearrange("a p c -> p a c").bitcast(I32))
-        table = [placed([P, T], U32, "table%d" % a, 8 + 19 * a) for a in range(PASSES)]
+        table = [placed([P, T], U32, "table%d" % a, 15 + 22 * a) for a in range(PASSES)]
         for a in range(PASSES):
             nc.sync.dma_start(table[a][:].bitcast(I32), tab_words[a].rearrange("p t i -> p (t i)").bitcast(I32))
 
-        we_raw_scales = kept([P, PASSES, H], U8, "we_raw_scales")
-        nc.gpsimd.memset(we_raw_scales[:].bitcast(I32), 0)
-        for q in range(QUADS):
-            nc.gpsimd.dma_start(we_raw_scales[32 * q:32 * q + 4].bitcast(I32),
-                                we_scales[:, 4 * q:4 * q + 4, :].rearrange("a r c -> r a c").bitcast(I32))
-
         picked_rows = kept([P, S], U8, "picked_rows")
         nc.vector.tensor_copy(picked_rows[:], scale_rows[:].indirect(offs_sb[:]))
-        v_scales = [kept([P, S], U8, "v_scales%d" % a) for a in range(PASSES)]
+        joint_rows = kept([P, S + H], U8, "joint_rows")
+        nc.vector.tensor_copy(joint_rows[:, S:].rearrange("p (t m) -> p m t", t=PACK),
+                              we_scale_rows[:].rearrange("p (m t) -> p m t", t=PACK))
+        nc.vector.tensor_copy(joint_rows[0:32, 0:S].bitcast(I32), picked_rows[0:32, :].bitcast(I32))
+        planes = [kept([P, S + H], U8, "planes%d" % a) for a in range(PASSES)]
         for a in range(PASSES):
-            nc.vector.memset(v_scales[a][:].bitcast(I32), 0)
-        for q in range(QUADS):
-            for a in range(PASSES):
-                queue = nc.scalar if q < QUADS - 1 else nc.gpsimd
+            nc.vector.memset(planes[a][:].bitcast(I32), 0)
+        for a in range(PASSES):
+            for q in range(QUADS):
                 row = 16 * a + 4 * q
-                queue.dma_start(v_scales[a][32 * q:32 * q + 4, :].bitcast(I32), picked_rows[row:row + 4, :].bitcast(I32))
+                nc.scalar.dma_start(planes[a][32 * q:32 * q + 4, :].bitcast(I32), joint_rows[row:row + 4, :].bitcast(I32))
 
         we_codes = kept([P, PASSES, 2 * H], U8, "we_codes")
         nc.vector.tensor_copy(we_codes[:].rearrange("p a (t m b) -> p a m t b", t=PACK, b=2),
@@ -84,10 +85,6 @@ def tile_list_phage_host_lysis_kernel(tc, tab_words, tab_scales, offs, offs2, of
         v_codes = [kept([P, S], U32, "v_codes%d" % a) for a in range(PASSES)]
         for a in range(PASSES):
             nc.vector.tensor_copy(v_codes[a][:], table[a][:].indirect(offs_sb[:]))
-
-        we_planes = placed([P, PASSES, H], U8, "we_planes", 18)
-        nc.vector.tensor_copy(we_planes[:].rearrange("p a (t m) -> p a m t", t=PACK),
-                              we_raw_scales[:].rearrange("p a (m t) -> p a m t", t=PACK))
 
         def load_weight(w, a, name, kib):
             raw = placed([P, PACK * H], F32, name, kib)
@@ -97,27 +94,27 @@ def tile_list_phage_host_lysis_kernel(tc, tab_words, tab_scales, offs, offs2, of
         wb_raw = [load_weight(wb, 0, "wb_raw0", 0), load_weight(wb, 1, "wb_raw1", 8)]
         wgb_sb = placed([P, M], F32, "wgb_sb", 16)
         nc.sync.dma_start(wgb_sb[:], wgb)
-        wp_raw = [load_weight(wp, 0, "wp_raw0", 19), load_weight(wp, 1, "wp_raw1", 27)]
-        bp_sb = placed([P, PACK], F32, "bp_sb", 35)
+        wp_raw = [load_weight(wp, 0, "wp_raw0", 18), load_weight(wp, 1, "wp_raw1", 29)]
+        bp_sb = placed([P, PACK], F32, "bp_sb", 28)
         nc.sync.dma_start(bp_sb[:], bp.rearrange("(p t) -> p t", t=PACK))
-        wga_sb = placed([P, M], F32, "wga_sb", 36)
+        wga_sb = placed([P, M], F32, "wga_sb", 26)
         nc.sync.dma_start(wga_sb[:], wga)
-        wy_codes = placed([P, N], U32, "wy_codes", 38)
+        wy_codes = placed([P, N], U32, "wy_codes", 37)
         nc.sync.dma_start(wy_codes[:].bitcast(I32), wy_words[0].rearrange("p c i -> p (c i)").bitcast(I32))
-        by_sb = placed([P, N_TILES], F32, "by_sb", 41)
+        by_sb = placed([P, N_TILES], F32, "by_sb", 40)
         with nc.allow_non_contiguous_dma(reason="one bias value for each output row"):
             nc.sync.dma_start(by_sb[:], by.rearrange("(j p) -> p j", p=P))
-        wy_plane = placed([P, N], U8, "wy_plane", 42)
+        wy_plane = placed([P, N], U8, "wy_plane", 41)
         nc.gpsimd.memset(wy_plane[:].bitcast(I32), 0)
         for q in range(QUADS):
-            nc.gpsimd.dma_start(wy_plane[32 * q:32 * q + 4, :].bitcast(I32), wy_scales[0, 4 * q:4 * q + 4, :].bitcast(I32))
+            nc.sync.dma_start(wy_plane[32 * q:32 * q + 4, :].bitcast(I32), wy_scales[0, 4 * q:4 * q + 4, :].bitcast(I32))
 
-        def first_stage(codes, planes, dtype, t, h):
-            acc = psum.tile([P, BANK], F32, name="acc")
+        def first_stage(codes, scales, dtype, banks, t, h):
+            acc = psum.tile([P, BANK], F32, name=banks)
             cols = slice(BANK * h, BANK * (h + 1))
             for a in range(PASSES):
-                nc.tensor.matmul_mx(acc[:], lhsT=codes(a, t).bitcast(dtype), lhsT_scale=planes(a, t),
-                                    rhs=v_codes[a][:, cols].bitcast(FP8X4), rhs_scale=v_scales[a][:, cols],
+                nc.tensor.matmul_mx(acc[:], lhsT=codes(a, t).bitcast(dtype), lhsT_scale=scales(a, t),
+                                    rhs=v_codes[a][:, cols].bitcast(FP8X4), rhs_scale=planes[a][:, cols],
                                     start=(a == 0), stop=(a == PASSES - 1))
             return acc, cols
 
@@ -133,35 +130,42 @@ def tile_list_phage_host_lysis_kernel(tc, tab_words, tab_scales, offs, offs2, of
                                       rounded[:, PACK * P * t:PACK * P * (t + 1)])
             return codes, plane
 
-        eb = [kept([P, S], F32, "eb%d" % t) for t in range(PACK)]
-        for t in range(PACK):
-            for h in range(HALVES):
-                acc, cols = first_stage(lambda a, t: we_codes[:, a, 2 * P * t:2 * P * (t + 1)],
-                                        lambda a, t: we_planes[:, a, P * t:P * (t + 1)], FP4X4, t, h)
-                nc.scalar.activation(eb[t][:, cols], acc[:], ACT.Exp)
-
         wb_mx = []
         for a in range(PASSES):
             rounded = kept([P, PACK * H], BF16, "wb_rounded%d" % a)
             round_weight(nc.vector.tensor_copy, wb_raw[a], rounded)
             wb_mx.append(quantise_weight(rounded, "wb%d" % a))
+        eb = [kept([P, S], F32, "eb%d" % t) for t in range(PACK)]
         hb = [kept([P, S], F32, "hb%d" % t) for t in range(PACK)]
-        for t in range(PACK):
+
+        def exp_rows(t):
+            for h in range(HALVES):
+                acc, cols = first_stage(lambda a, t: we_codes[:, a, 2 * P * t:2 * P * (t + 1)],
+                                        lambda a, t: planes[a][:, S + P * t:S + P * (t + 1)], FP4X4, "for_scalar", t, h)
+                nc.scalar.activation(eb[t][:, cols], acc[:], ACT.Exp)
+
+        def hb_rows(t):
             for h in range(HALVES):
                 acc, cols = first_stage(lambda a, t: wb_mx[a][0][:, P * t:P * (t + 1)],
-                                        lambda a, t: wb_mx[a][1][:, P * t:P * (t + 1)], FP8X4, t, h)
+                                        lambda a, t: wb_mx[a][1][:, P * t:P * (t + 1)], FP8X4, "other", t, h)
                 nc.vector.tensor_tensor(hb[t][:, cols], acc[:], eb[t][:, cols], ALU.mult)
+
+        exp_rows(0)
+        for t in range(1, PACK):
+            exp_rows(t)
+            hb_rows(t - 1)
+        hb_rows(PACK - 1)
 
         wp_mx = []
         for a in range(PASSES):
-            rounded = placed([P, PACK * H], BF16, "wp_rounded%d" % a, 43 + 4 * a)
+            rounded = placed([P, PACK * H], BF16, "wp_rounded%d" % a, 53 + 4 * a)
             round_weight(nc.scalar.copy, wp_raw[a], rounded)
             wp_mx.append(quantise_weight(rounded, "wp%d" % a))
         hp = [kept([P, S], F32, "hp%d" % t) for t in range(PACK)]
         for t in range(PACK):
             for h in range(HALVES):
                 acc, cols = first_stage(lambda a, t: wp_mx[a][0][:, P * t:P * (t + 1)],
-                                        lambda a, t: wp_mx[a][1][:, P * t:P * (t + 1)], FP8X4, t, h)
+                                        lambda a, t: wp_mx[a][1][:, P * t:P * (t + 1)], FP8X4, "for_scalar", t, h)
                 nc.scalar.activation(hp[t][:, cols], acc[:], ACT.Identity, bias=bp_sb[:, t:t + 1])
 
         def pick(picked, h_tiles, offsets, weights, m0, width):
@@ -172,7 +176,7 @@ def tile_list_phage_host_lysis_kernel(tc, tab_words, tab_scales, offs, offs2, of
         xb = []
         for piece, (m0, width) in enumerate(PIECES):
             if piece == 0:
-                picked = placed([P, PACK, width], F32, "xb0", 47)
+                picked = placed([P, PACK, width], F32, "xb0", 57)
             else:
                 picked = kept([P, PACK, width], F32, "xb%d" % piece)
             pick(picked, hb, offs3_sb, wgb_sb, m0, width)
@@ -180,7 +184,7 @@ def tile_list_phage_host_lysis_kernel(tc, tab_words, tab_scales, offs, offs2, of
 
         out_rows = out.rearrange("(j p) m -> p j m", p=P)
         for piece, (m0, width) in enumerate(PIECES):
-            xa = placed([P, PACK, width], F32, "xa%d" % piece, 53)
+            xa = placed([P, PACK, width], F32, "xa%d" % piece, 63)
             pick(xa, hp, offs2_sb, wga_sb, m0, width)
             z = kept([P, PACK * width], BF16, "z%d" % piece)
             nc.vector.tensor_tensor(z[:].rearrange("p (c i t) -> p c t i", i=4, t=PACK),
@@ -191,7 +195,7 @@ def tile_list_phage_host_lysis_kernel(tc, tab_words, tab_scales, offs, offs2, of
             nc.vector.quantize_mx(z_codes[:].bitcast(FP8X4), z_plane[:], z[:])
             scores = kept([P, N_TILES, width], F32, "scores%d" % piece)
             for j in range(N_TILES):
-                acc = psum.tile([P, BANK], F32, name="acc")
+                acc = psum.tile([P, BANK], F32, name="other")
                 for c0 in range(0, width, 256):
                     cols = slice(c0, min(c0 + 256, width))
                     nc.tensor.matmul_mx(acc[:, cols], lhsT=wy_codes[:, P * j:P * (j + 1)].bitcast(FP8X4),

@@ -18,14 +18,33 @@ ALU = mybir.AluOpType
 
 P = 128
 PACK = 4
-PASSES = K // (P * PACK)
+K_PASS = P * PACK
+PASSES = K // K_PASS
+BLOCKS = 16
+QUADRANT = 32
 BANK = 512
 HALVES = S // BANK
 N_TILES = N // P
-QUADS = 4
+LIST_ROWS = 16
 KIB = 1024
+
 PIECES = ((0, 384), (384, 128))
+MAX_MOVING = 256
 STORE_TILES = 2
+EXP_LEAD = 2
+
+PAIRS = 4
+EXP_PAIRS = (0, 1, 2, 0)
+HB_PAIRS = (3, 1, 3, 1)
+HP_PAIRS = (2, 0, 3, 1)
+
+AT_SCALE_ROWS = 0
+AT_TABLE = (4, 27)
+AT_WB = (0, 8)
+AT_WGB = 16
+AT_WP = (20, 42)
+AT_BP, AT_WGA, AT_WY, AT_BY, AT_WY_PLANE = 28, 29, 31, 34, 35
+AT_XA = 50
 
 
 def tile_list_phage_host_lysis_kernel(tc, tab_words, tab_scales, offs, offs2, offs3, wp, bp, wb,
@@ -35,33 +54,35 @@ def tile_list_phage_host_lysis_kernel(tc, tab_words, tab_scales, offs, offs2, of
         lists = ctx.enter_context(tc.tile_pool(name="lists", bufs=1))
         keep = ctx.enter_context(tc.tile_pool(name="keep", bufs=1))
         shared = ctx.enter_context(tc.tile_pool(name="shared", bufs=1))
-        psum = ctx.enter_context(tc.psum_pool(name="psum", bufs=4))
-
-        def placed(shape, dtype, name, kib):
-            return shared.tile(shape, dtype, name=name, offset=kib * KIB, align_bytes=64)
+        psum = ctx.enter_context(tc.psum_pool(name="psum", bufs=HALVES))
 
         def kept(shape, dtype, name):
             return keep.tile(shape, dtype, name=name, align_bytes=64)
 
-        offs_sb = lists.tile([P, S // 16], U16, name="offs_sb")
-        offs2_sb = lists.tile([P, M // 16], U16, name="offs2_sb")
-        offs3_sb = lists.tile([P, M // 16], U16, name="offs3_sb")
-        nc.sync.dma_start(offs_sb[:], offs)
+        def placed(shape, dtype, name, kib):
+            return shared.tile(shape, dtype, name=name, offset=kib * KIB, align_bytes=64)
 
-        scale_rows = placed([P, T], U8, "scale_rows", 0)
-        nc.sync.dma_start(scale_rows[0:32, :].bitcast(I32), tab_scales.rearrange("a q t -> (a q) t").bitcast(I32))
-        nc.vector.memset(scale_rows[32:64, :].bitcast(I32), 0)
-        nc.vector.memset(scale_rows[64:128, :].bitcast(I32), 0)
+        def bank(pair):
+            return psum.tile([P, BANK], F32, name="pair%d" % pair)
+
+        def load_scale_rows(rows, scales):
+            nc.sync.dma_start(rows[0:QUADRANT, :].bitcast(I32), scales.rearrange("a b c -> (a b) c").bitcast(I32))
+            nc.vector.memset(rows[QUADRANT:2 * QUADRANT, :].bitcast(I32), 0)
+            nc.vector.memset(rows[2 * QUADRANT:P, :].bitcast(I32), 0)
+
+        offs_sb = lists.tile([P, S // LIST_ROWS], U16, name="offs_sb")
+        offs2_sb = lists.tile([P, M // LIST_ROWS], U16, name="offs2_sb")
+        offs3_sb = lists.tile([P, M // LIST_ROWS], U16, name="offs3_sb")
+        table = [placed([P, T], U32, "table%d" % a, AT_TABLE[a]) for a in range(PASSES)]
+        nc.sync.dma_start(offs_sb[:], offs)
+        scale_rows = placed([P, T], U8, "scale_rows", AT_SCALE_ROWS)
+        load_scale_rows(scale_rows, tab_scales)
         we_scale_rows = kept([P, H], U8, "we_scale_rows")
-        nc.sync.dma_start(we_scale_rows[0:32, :].bitcast(I32), we_scales.rearrange("a q c -> (a q) c").bitcast(I32))
-        nc.vector.memset(we_scale_rows[32:64, :].bitcast(I32), 0)
-        nc.vector.memset(we_scale_rows[64:128, :].bitcast(I32), 0)
+        load_scale_rows(we_scale_rows, we_scales)
         nc.sync.dma_start(offs3_sb[:], offs3)
         nc.sync.dma_start(offs2_sb[:], offs2)
-
         we_raw = kept([P, PASSES, 2 * H], U8, "we_raw")
         nc.sync.dma_start(we_raw[:].bitcast(I32), we_words.rearrange("a p c -> p a c").bitcast(I32))
-        table = [placed([P, T], U32, "table%d" % a, 15 + 22 * a) for a in range(PASSES)]
         for a in range(PASSES):
             nc.sync.dma_start(table[a][:].bitcast(I32), tab_words[a].rearrange("p t i -> p (t i)").bitcast(I32))
 
@@ -70,134 +91,144 @@ def tile_list_phage_host_lysis_kernel(tc, tab_words, tab_scales, offs, offs2, of
         joint_rows = kept([P, S + H], U8, "joint_rows")
         nc.vector.tensor_copy(joint_rows[:, S:].rearrange("p (t m) -> p m t", t=PACK),
                               we_scale_rows[:].rearrange("p (m t) -> p m t", t=PACK))
-        nc.vector.tensor_copy(joint_rows[0:32, 0:S].bitcast(I32), picked_rows[0:32, :].bitcast(I32))
+        nc.vector.tensor_copy(joint_rows[0:QUADRANT, 0:S].bitcast(I32), picked_rows[0:QUADRANT, :].bitcast(I32))
         planes = [kept([P, S + H], U8, "planes%d" % a) for a in range(PASSES)]
         for a in range(PASSES):
             nc.vector.memset(planes[a][:].bitcast(I32), 0)
         for a in range(PASSES):
-            for q in range(QUADS):
-                row = 16 * a + 4 * q
-                nc.scalar.dma_start(planes[a][32 * q:32 * q + 4, :].bitcast(I32), joint_rows[row:row + 4, :].bitcast(I32))
+            for r in range(PACK):
+                nc.scalar.dma_start(planes[a][r:P:QUADRANT, :].bitcast(I32),
+                                    joint_rows[BLOCKS * a + r:BLOCKS * (a + 1):PACK, :].bitcast(I32))
 
         we_codes = kept([P, PASSES, 2 * H], U8, "we_codes")
-        nc.vector.tensor_copy(we_codes[:].rearrange("p a (t m b) -> p a m t b", t=PACK, b=2),
-                              we_raw[:].rearrange("p a (m t b) -> p a m t b", t=PACK, b=2))
+        nc.vector.tensor_copy(we_codes[:].bitcast(U16).rearrange("p a (t m) -> p a m t", t=PACK),
+                              we_raw[:].bitcast(U16).rearrange("p a (m t) -> p a m t", t=PACK))
         v_codes = [kept([P, S], U32, "v_codes%d" % a) for a in range(PASSES)]
         for a in range(PASSES):
             nc.vector.tensor_copy(v_codes[a][:], table[a][:].indirect(offs_sb[:]))
 
         def load_weight(w, a, name, kib):
             raw = placed([P, PACK * H], F32, name, kib)
-            nc.sync.dma_start(raw[:], w[512 * a:512 * (a + 1), :].rearrange("(p j) c -> p (j c)", j=PACK))
+            nc.sync.dma_start(raw[:], w[K_PASS * a:K_PASS * (a + 1), :].rearrange("(p j) c -> p (j c)", j=PACK))
             return raw
 
-        wb_raw = [load_weight(wb, 0, "wb_raw0", 0), load_weight(wb, 1, "wb_raw1", 8)]
-        wgb_sb = placed([P, M], F32, "wgb_sb", 16)
+        wb_raw = [load_weight(wb, a, "wb_raw%d" % a, AT_WB[a]) for a in range(PASSES)]
+        wgb_sb = placed([P, M], F32, "wgb_sb", AT_WGB)
         nc.sync.dma_start(wgb_sb[:], wgb)
-        wp_raw = [load_weight(wp, 0, "wp_raw0", 18), load_weight(wp, 1, "wp_raw1", 29)]
-        bp_sb = placed([P, PACK], F32, "bp_sb", 28)
+        wp_raw = [load_weight(wp, a, "wp_raw%d" % a, AT_WP[a]) for a in range(PASSES)]
+        bp_sb = placed([P, PACK], F32, "bp_sb", AT_BP)
         nc.sync.dma_start(bp_sb[:], bp.rearrange("(p t) -> p t", t=PACK))
-        wga_sb = placed([P, M], F32, "wga_sb", 26)
+        wga_sb = placed([P, M], F32, "wga_sb", AT_WGA)
         nc.sync.dma_start(wga_sb[:], wga)
-        wy_codes = placed([P, N], U32, "wy_codes", 37)
+        wy_codes = placed([P, N], U32, "wy_codes", AT_WY)
         nc.sync.dma_start(wy_codes[:].bitcast(I32), wy_words[0].rearrange("p c i -> p (c i)").bitcast(I32))
-        by_sb = placed([P, N_TILES], F32, "by_sb", 40)
+        by_sb = placed([P, N_TILES], F32, "by_sb", AT_BY)
         with nc.allow_non_contiguous_dma(reason="one bias value for each output row"):
             nc.sync.dma_start(by_sb[:], by.rearrange("(j p) -> p j", p=P))
-        wy_plane = placed([P, N], U8, "wy_plane", 41)
+        wy_plane = placed([P, N], U8, "wy_plane", AT_WY_PLANE)
         nc.gpsimd.memset(wy_plane[:].bitcast(I32), 0)
-        for q in range(QUADS):
-            nc.sync.dma_start(wy_plane[32 * q:32 * q + 4, :].bitcast(I32), wy_scales[0, 4 * q:4 * q + 4, :].bitcast(I32))
+        for q in range(P // QUADRANT):
+            nc.sync.dma_start(wy_plane[QUADRANT * q:QUADRANT * q + PACK, :].bitcast(I32),
+                              wy_scales[0, PACK * q:PACK * (q + 1), :].bitcast(I32))
 
-        def first_stage(codes, scales, dtype, banks, t, h):
-            acc = psum.tile([P, BANK], F32, name=banks)
+        def first_stage(codes, scales, dtype, pair, h):
+            acc = bank(pair)
             cols = slice(BANK * h, BANK * (h + 1))
             for a in range(PASSES):
-                nc.tensor.matmul_mx(acc[:], lhsT=codes(a, t).bitcast(dtype), lhsT_scale=scales(a, t),
+                nc.tensor.matmul_mx(acc[:], lhsT=codes[a].bitcast(dtype), lhsT_scale=scales[a],
                                     rhs=v_codes[a][:, cols].bitcast(FP8X4), rhs_scale=planes[a][:, cols],
                                     start=(a == 0), stop=(a == PASSES - 1))
             return acc, cols
 
-        def round_weight(copy, raw, rounded):
-            copy(rounded[:].rearrange("p (t m j) -> p m j t", t=PACK, j=PACK),
-                 raw[:].rearrange("p (j m t) -> p m j t", t=PACK, j=PACK))
+        def by_slices(raw):
+            return raw[:].rearrange("p (j m t) -> p m j t", t=PACK, j=PACK)
 
-        def quantise_weight(rounded, name):
-            codes = kept([P, H], U32, name + "_codes")
-            plane = kept([P, H], U8, name + "_plane")
-            for t in range(PACK):
-                nc.vector.quantize_mx(codes[:, P * t:P * (t + 1)].bitcast(FP8X4), plane[:, P * t:P * (t + 1)],
-                                      rounded[:, PACK * P * t:PACK * P * (t + 1)])
-            return codes, plane
+        def as_words(rounded):
+            return rounded.rearrange("p (t m j) -> p m j t", m=P, j=PACK)
 
-        wb_mx = []
-        for a in range(PASSES):
-            rounded = kept([P, PACK * H], BF16, "wb_rounded%d" % a)
-            round_weight(nc.vector.tensor_copy, wb_raw[a], rounded)
-            wb_mx.append(quantise_weight(rounded, "wb%d" % a))
+        def mx_tiles(name):
+            return kept([P, H], U32, name + "_codes"), kept([P, H], U8, name + "_plane")
+
+        def quantise(mx, rounded, t0, t1):
+            cols = slice(P * t0, P * t1)
+            nc.vector.quantize_mx(mx[0][:, cols].bitcast(FP8X4), mx[1][:, cols], rounded)
+
+        def slice_of(mx, t):
+            return [codes[:, P * t:P * (t + 1)] for codes, plane in mx], [plane[:, P * t:P * (t + 1)] for codes, plane in mx]
+
+        wb_mx = [mx_tiles("wb%d" % a) for a in range(PASSES)]
+        wb_rounded = kept([P, PACK * H], BF16, "wb_rounded")
+        nc.vector.tensor_copy(as_words(wb_rounded[:]), by_slices(wb_raw[0]))
+        quantise(wb_mx[0], wb_rounded[:], 0, PACK)
+        for t0 in range(0, PACK, 2):
+            wb_two_slices = kept([P, 2 * H], BF16, "wb_two_slices")
+            nc.vector.tensor_copy(as_words(wb_two_slices[:]), by_slices(wb_raw[1])[:, :, :, t0:t0 + 2])
+            quantise(wb_mx[1], wb_two_slices[:], t0, t0 + 2)
+
         eb = [kept([P, S], F32, "eb%d" % t) for t in range(PACK)]
         hb = [kept([P, S], F32, "hb%d" % t) for t in range(PACK)]
 
-        def exp_rows(t):
+        def exp_slice(t):
+            codes = [we_codes[:, a, 2 * P * t:2 * P * (t + 1)] for a in range(PASSES)]
+            scales = [planes[a][:, S + P * t:S + P * (t + 1)] for a in range(PASSES)]
             for h in range(HALVES):
-                acc, cols = first_stage(lambda a, t: we_codes[:, a, 2 * P * t:2 * P * (t + 1)],
-                                        lambda a, t: planes[a][:, S + P * t:S + P * (t + 1)], FP4X4, "for_scalar", t, h)
+                acc, cols = first_stage(codes, scales, FP4X4, EXP_PAIRS[t], h)
                 nc.scalar.activation(eb[t][:, cols], acc[:], ACT.Exp)
 
-        def hb_rows(t):
+        def hb_slice(t):
+            codes, scales = slice_of(wb_mx, t)
             for h in range(HALVES):
-                acc, cols = first_stage(lambda a, t: wb_mx[a][0][:, P * t:P * (t + 1)],
-                                        lambda a, t: wb_mx[a][1][:, P * t:P * (t + 1)], FP8X4, "other", t, h)
+                acc, cols = first_stage(codes, scales, FP8X4, HB_PAIRS[t], h)
                 nc.vector.tensor_tensor(hb[t][:, cols], acc[:], eb[t][:, cols], ALU.mult)
 
-        exp_rows(0)
-        for t in range(1, PACK):
-            exp_rows(t)
-            hb_rows(t - 1)
-        hb_rows(PACK - 1)
+        for step in range(PACK + EXP_LEAD):
+            if step < PACK:
+                exp_slice(step)
+            if step >= EXP_LEAD:
+                hb_slice(step - EXP_LEAD)
 
-        wp_mx = []
-        for a in range(PASSES):
-            rounded = placed([P, PACK * H], BF16, "wp_rounded%d" % a, 53 + 4 * a)
-            round_weight(nc.scalar.copy, wp_raw[a], rounded)
-            wp_mx.append(quantise_weight(rounded, "wp%d" % a))
+        wp_mx = [mx_tiles("wp%d" % a) for a in range(PASSES)]
+        xb = kept([P, PACK * M], F32, "xb")
+        wp_rounded = kept([P, PACK * H], BF16, "wp_rounded")
+        borrowed = xb[:, 3 * M // 2:7 * M // 2].bitcast(BF16)
+        for a, rounded in enumerate((wp_rounded[:], borrowed)):
+            for m0 in range(0, P, P // 2):
+                nc.scalar.copy(as_words(rounded)[:, m0:m0 + P // 2], by_slices(wp_raw[a])[:, m0:m0 + P // 2])
+            width = PACK // (a + 1)
+            for t0 in range(0, PACK, width):
+                quantise(wp_mx[a], rounded[:, K_PASS * t0:K_PASS * (t0 + width)], t0, t0 + width)
         hp = [kept([P, S], F32, "hp%d" % t) for t in range(PACK)]
         for t in range(PACK):
+            codes, scales = slice_of(wp_mx, t)
             for h in range(HALVES):
-                acc, cols = first_stage(lambda a, t: wp_mx[a][0][:, P * t:P * (t + 1)],
-                                        lambda a, t: wp_mx[a][1][:, P * t:P * (t + 1)], FP8X4, "for_scalar", t, h)
+                acc, cols = first_stage(codes, scales, FP8X4, HP_PAIRS[t], h)
                 nc.scalar.activation(hp[t][:, cols], acc[:], ACT.Identity, bias=bp_sb[:, t:t + 1])
 
-        def pick(picked, h_tiles, offsets, weights, m0, width):
+        def pick(picked, h_slices, offsets, weights, m0, width):
+            entries = offsets[:, m0 // LIST_ROWS:(m0 + width) // LIST_ROWS]
             for t in range(PACK):
-                nc.vector.tensor_tensor(picked[:, t, :], h_tiles[t][:].indirect(offsets[:, m0 // 16:(m0 + width) // 16]),
+                nc.vector.tensor_tensor(picked[:, t, :], h_slices[t][:].indirect(entries),
                                         weights[:, m0:m0 + width], ALU.mult)
 
-        xb = []
-        for piece, (m0, width) in enumerate(PIECES):
-            if piece == 0:
-                picked = placed([P, PACK, width], F32, "xb0", 57)
-            else:
-                picked = kept([P, PACK, width], F32, "xb%d" % piece)
-            pick(picked, hb, offs3_sb, wgb_sb, m0, width)
-            xb.append(picked)
+        xb_slices = xb[:].rearrange("p (t m) -> p t m", t=PACK)
+        pick(xb_slices, hb, offs3_sb, wgb_sb, 0, M)
 
         out_rows = out.rearrange("(j p) m -> p j m", p=P)
         for piece, (m0, width) in enumerate(PIECES):
-            xa = placed([P, PACK, width], F32, "xa%d" % piece, 63)
+            xa = placed([P, PACK, width], F32, "xa%d" % piece, AT_XA)
             pick(xa, hp, offs2_sb, wga_sb, m0, width)
             z = kept([P, PACK * width], BF16, "z%d" % piece)
             nc.vector.tensor_tensor(z[:].rearrange("p (c i t) -> p c t i", i=4, t=PACK),
                                     xa[:].rearrange("p t (c i) -> p c t i", i=4),
-                                    xb[piece][:].rearrange("p t (c i) -> p c t i", i=4), ALU.max)
+                                    xb_slices[:, :, m0:m0 + width].rearrange("p t (c i) -> p c t i", i=4), ALU.max)
             z_codes = kept([P, width], U32, "z_codes%d" % piece)
             z_plane = kept([P, width], U8, "z_plane%d" % piece)
             nc.vector.quantize_mx(z_codes[:].bitcast(FP8X4), z_plane[:], z[:])
             scores = kept([P, N_TILES, width], F32, "scores%d" % piece)
             for j in range(N_TILES):
-                acc = psum.tile([P, BANK], F32, name="other")
-                for c0 in range(0, width, 256):
-                    cols = slice(c0, min(c0 + 256, width))
+                acc = bank(j % PAIRS)
+                for c0 in range(0, width, MAX_MOVING):
+                    cols = slice(c0, min(c0 + MAX_MOVING, width))
                     nc.tensor.matmul_mx(acc[:, cols], lhsT=wy_codes[:, P * j:P * (j + 1)].bitcast(FP8X4),
                                         lhsT_scale=wy_plane[:, P * j:P * (j + 1)],
                                         rhs=z_codes[:, cols].bitcast(FP8X4), rhs_scale=z_plane[:, cols],

@@ -89,8 +89,8 @@ def tile_list_phage_host_lysis_kernel(tc, tab_words, tab_scales, offs, offs2, of
         picked_rows = kept([P, S], U8, "picked_rows")
         nc.vector.tensor_copy(picked_rows[:], scale_rows[:].indirect(offs_sb[:]))
         joint_rows = kept([P, S + H], U8, "joint_rows")
-        nc.vector.tensor_copy(joint_rows[:, S:].rearrange("p (t m) -> p m t", t=PACK),
-                              we_scale_rows[:].rearrange("p (m t) -> p m t", t=PACK))
+        nc.vector.tensor_copy(joint_rows[:, S:].rearrange("p (t m) -> p t m", t=PACK),
+                              we_scale_rows[:].rearrange("p (m t) -> p t m", t=PACK))
         nc.vector.tensor_copy(joint_rows[0:QUADRANT, 0:S].bitcast(I32), picked_rows[0:QUADRANT, :].bitcast(I32))
         planes = [kept([P, S + H], U8, "planes%d" % a) for a in range(PASSES)]
         for a in range(PASSES):
@@ -101,8 +101,8 @@ def tile_list_phage_host_lysis_kernel(tc, tab_words, tab_scales, offs, offs2, of
                                     joint_rows[BLOCKS * a + r:BLOCKS * (a + 1):PACK, :].bitcast(I32))
 
         we_codes = kept([P, PASSES, 2 * H], U8, "we_codes")
-        nc.vector.tensor_copy(we_codes[:].bitcast(U16).rearrange("p a (t m) -> p a m t", t=PACK),
-                              we_raw[:].bitcast(U16).rearrange("p a (m t) -> p a m t", t=PACK))
+        nc.vector.tensor_copy(we_codes[:].bitcast(U16).rearrange("p a (t m) -> p a t m", t=PACK),
+                              we_raw[:].bitcast(U16).rearrange("p a (m t) -> p a t m", t=PACK))
         v_codes = [kept([P, S], U32, "v_codes%d" % a) for a in range(PASSES)]
         for a in range(PASSES):
             nc.vector.tensor_copy(v_codes[a][:], table[a][:].indirect(offs_sb[:]))
@@ -141,29 +141,29 @@ def tile_list_phage_host_lysis_kernel(tc, tab_words, tab_scales, offs, offs2, of
             return acc, cols
 
         def by_slices(raw):
-            return raw[:].rearrange("p (j m t) -> p m j t", t=PACK, j=PACK)
+            return raw[:].rearrange("p (j m t) -> p m t j", t=PACK, j=PACK)
 
         def as_words(rounded):
-            return rounded.rearrange("p (t m j) -> p m j t", m=P, j=PACK)
+            return rounded.rearrange("p (t m j) -> p m t j", t=PACK, j=PACK)
 
         def mx_tiles(name):
             return kept([P, H], U32, name + "_codes"), kept([P, H], U8, name + "_plane")
 
-        def quantise(mx, rounded, t0, t1):
-            cols = slice(P * t0, P * t1)
-            nc.vector.quantize_mx(mx[0][:, cols].bitcast(FP8X4), mx[1][:, cols], rounded)
-
         def slice_of(mx, t):
             return [codes[:, P * t:P * (t + 1)] for codes, plane in mx], [plane[:, P * t:P * (t + 1)] for codes, plane in mx]
 
+        def quantise_pass(mx, a, rounded):
+            width = PACK // (a + 1)
+            for t0 in range(0, PACK, width):
+                cols = slice(P * t0, P * (t0 + width))
+                nc.vector.quantize_mx(mx[a][0][:, cols].bitcast(FP8X4), mx[a][1][:, cols],
+                                      rounded[:, K_PASS * t0:K_PASS * (t0 + width)])
+
         wb_mx = [mx_tiles("wb%d" % a) for a in range(PASSES)]
-        wb_rounded = kept([P, PACK * H], BF16, "wb_rounded")
-        nc.vector.tensor_copy(as_words(wb_rounded[:]), by_slices(wb_raw[0]))
-        quantise(wb_mx[0], wb_rounded[:], 0, PACK)
-        for t0 in range(0, PACK, 2):
-            wb_two_slices = kept([P, 2 * H], BF16, "wb_two_slices")
-            nc.vector.tensor_copy(as_words(wb_two_slices[:]), by_slices(wb_raw[1])[:, :, :, t0:t0 + 2])
-            quantise(wb_mx[1], wb_two_slices[:], t0, t0 + 2)
+        for a in range(PASSES):
+            wb_rounded = kept([P, PACK * H], BF16, "wb_rounded%d" % a)
+            nc.vector.tensor_copy(as_words(wb_rounded[:]), by_slices(wb_raw[a]))
+            quantise_pass(wb_mx, a, wb_rounded[:])
 
         eb = [kept([P, S], F32, "eb%d" % t) for t in range(PACK)]
         hb = [kept([P, S], F32, "hb%d" % t) for t in range(PACK)]
@@ -194,9 +194,7 @@ def tile_list_phage_host_lysis_kernel(tc, tab_words, tab_scales, offs, offs2, of
         for a, rounded in enumerate((wp_rounded[:], borrowed)):
             for m0 in range(0, P, P // 2):
                 nc.scalar.copy(as_words(rounded)[:, m0:m0 + P // 2], by_slices(wp_raw[a])[:, m0:m0 + P // 2])
-            width = PACK // (a + 1)
-            for t0 in range(0, PACK, width):
-                quantise(wp_mx[a], rounded[:, K_PASS * t0:K_PASS * (t0 + width)], t0, t0 + width)
+            quantise_pass(wp_mx, a, rounded)
         hp = [kept([P, S], F32, "hp%d" % t) for t in range(PACK)]
         for t in range(PACK):
             codes, scales = slice_of(wp_mx, t)
@@ -218,9 +216,9 @@ def tile_list_phage_host_lysis_kernel(tc, tab_words, tab_scales, offs, offs2, of
             xa = placed([P, PACK, width], F32, "xa%d" % piece, AT_XA)
             pick(xa, hp, offs2_sb, wga_sb, m0, width)
             z = kept([P, PACK * width], BF16, "z%d" % piece)
-            nc.vector.tensor_tensor(z[:].rearrange("p (c i t) -> p c t i", i=4, t=PACK),
-                                    xa[:].rearrange("p t (c i) -> p c t i", i=4),
-                                    xb_slices[:, :, m0:m0 + width].rearrange("p t (c i) -> p c t i", i=4), ALU.max)
+            nc.vector.tensor_tensor(z[:].rearrange("p (c i t) -> p c t i", i=2, t=PACK),
+                                    xa[:].rearrange("p t (c i) -> p c t i", i=2),
+                                    xb_slices[:, :, m0:m0 + width].rearrange("p t (c i) -> p c t i", i=2), ALU.max)
             z_codes = kept([P, width], U32, "z_codes%d" % piece)
             z_plane = kept([P, width], U8, "z_plane%d" % piece)
             nc.vector.quantize_mx(z_codes[:].bitcast(FP8X4), z_plane[:], z[:])

from contextlib import ExitStack

import concourse.mybir as mybir

K, H, N, T, S, M = 1024, 512, 768, 4096, 1024, 512
FLOPS = 2 * (3 * K * H * S + H * N * M)

F32 = mybir.dt.float32
BF16 = mybir.dt.bfloat16
I32 = mybir.dt.int32
U32 = mybir.dt.uint32
U16 = mybir.dt.uint16
U8 = mybir.dt.uint8
FP8X4 = mybir.dt.float8_e4m3fn_x4
FP4X4 = mybir.dt.float4_e2m1fn_x4
ACT = mybir.ActivationFunctionType
ALU = mybir.AluOpType

P = 128
PACK = 4
K_PASS = P * PACK
PASSES = K // K_PASS
BLOCKS = 16
QUADRANT = 32
BANK = 512
HALVES = S // BANK
N_TILES = N // P
LIST_ROWS = 16
KIB = 1024

PIECES = ((0, 384), (384, 128))
MAX_MOVING = 256
STORE_TILES = 2
EXP_LEAD = 2

PAIRS = 4
EXP_PAIRS = (0, 1, 2, 0)
HB_PAIRS = (3, 1, 3, 1)
HP_PAIRS = (2, 0, 3, 1)

AT_SCALE_ROWS = 0
AT_TABLE = (4, 27)
AT_WB = (0, 8)
AT_WGB = 16
AT_WP = (20, 42)
AT_BP, AT_WGA, AT_WY, AT_BY, AT_WY_PLANE = 28, 29, 31, 34, 35
AT_XA = 50


def tile_list_phage_host_lysis_kernel(tc, tab_words, tab_scales, offs, offs2, offs3, wp, bp, wb,
                                                we_words, we_scales, wga, wgb, wy_words, wy_scales, by, out):
    nc = tc.nc
    with ExitStack() as ctx:
        lists = ctx.enter_context(tc.tile_pool(name="lists", bufs=1))
        keep = ctx.enter_context(tc.tile_pool(name="keep", bufs=1))
        shared = ctx.enter_context(tc.tile_pool(name="shared", bufs=1))
        psum = ctx.enter_context(tc.psum_pool(name="psum", bufs=HALVES))

        def kept(shape, dtype, name):
            return keep.tile(shape, dtype, name=name, align_bytes=64)

        def placed(shape, dtype, name, kib):
            return shared.tile(shape, dtype, name=name, offset=kib * KIB, align_bytes=64)

        def bank(pair):
            return psum.tile([P, BANK], F32, name="pair%d" % pair)

        def load_scale_rows(rows, scales):
            nc.sync.dma_start(rows[0:QUADRANT, :].bitcast(I32), scales.rearrange("a b c -> (a b) c").bitcast(I32))
            nc.vector.memset(rows[QUADRANT:2 * QUADRANT, :].bitcast(I32), 0)
            nc.vector.memset(rows[2 * QUADRANT:P, :].bitcast(I32), 0)

        offs_sb = lists.tile([P, S // LIST_ROWS], U16, name="offs_sb")
        offs2_sb = lists.tile([P, M // LIST_ROWS], U16, name="offs2_sb")
        offs3_sb = lists.tile([P, M // LIST_ROWS], U16, name="offs3_sb")
        table = [placed([P, T], U32, "table%d" % a, AT_TABLE[a]) for a in range(PASSES)]
        nc.sync.dma_start(offs_sb[:], offs)
        scale_rows = placed([P, T], U8, "scale_rows", AT_SCALE_ROWS)
        load_scale_rows(scale_rows, tab_scales)
        we_scale_rows = kept([P, H], U8, "we_scale_rows")
        load_scale_rows(we_scale_rows, we_scales)
        nc.sync.dma_start(offs3_sb[:], offs3)
        nc.sync.dma_start(offs2_sb[:], offs2)
        we_raw = kept([P, PASSES, 2 * H], U8, "we_raw")
        nc.sync.dma_start(we_raw[:].bitcast(I32), we_words.rearrange("a p c -> p a c").bitcast(I32))
        for a in range(PASSES):
            nc.sync.dma_start(table[a][:].bitcast(I32), tab_words[a].rearrange("p t i -> p (t i)").bitcast(I32))

        picked_rows = kept([P, S], U8, "picked_rows")
        nc.vector.tensor_copy(picked_rows[:], scale_rows[:].indirect(offs_sb[:]))
        joint_rows = kept([P, S + H], U8, "joint_rows")
        nc.vector.tensor_copy(joint_rows[:, S:].rearrange("p (t m) -> p t m", t=PACK),
                              we_scale_rows[:].rearrange("p (m t) -> p t m", t=PACK))
        nc.vector.tensor_copy(joint_rows[0:QUADRANT, 0:S].bitcast(I32), picked_rows[0:QUADRANT, :].bitcast(I32))
        planes = [kept([P, S + H], U8, "planes%d" % a) for a in range(PASSES)]
        for a in range(PASSES):
            nc.vector.memset(planes[a][:].bitcast(I32), 0)
        for a in range(PASSES):
            for r in range(PACK):
                nc.scalar.dma_start(planes[a][r:P:QUADRANT, :].bitcast(I32),
                                    joint_rows[BLOCKS * a + r:BLOCKS * (a + 1):PACK, :].bitcast(I32))

        we_codes = kept([P, PASSES, 2 * H], U8, "we_codes")
        nc.vector.tensor_copy(we_codes[:].bitcast(U16).rearrange("p a (t m) -> p a t m", t=PACK),
                              we_raw[:].bitcast(U16).rearrange("p a (m t) -> p a t m", t=PACK))
        v_codes = [kept([P, S], U32, "v_codes%d" % a) for a in range(PASSES)]
        for a in range(PASSES):
            nc.vector.tensor_copy(v_codes[a][:], table[a][:].indirect(offs_sb[:]))

        def load_weight(w, a, name, kib):
            raw = placed([P, PACK * H], F32, name, kib)
            nc.sync.dma_start(raw[:], w[K_PASS * a:K_PASS * (a + 1), :].rearrange("(p j) c -> p (j c)", j=PACK))
            return raw

        wb_raw = [load_weight(wb, a, "wb_raw%d" % a, AT_WB[a]) for a in range(PASSES)]
        wgb_sb = placed([P, M], F32, "wgb_sb", AT_WGB)
        nc.sync.dma_start(wgb_sb[:], wgb)
        wp_raw = [load_weight(wp, a, "wp_raw%d" % a, AT_WP[a]) for a in range(PASSES)]
        bp_sb = placed([P, PACK], F32, "bp_sb", AT_BP)
        nc.sync.dma_start(bp_sb[:], bp.rearrange("(p t) -> p t", t=PACK))
        wga_sb = placed([P, M], F32, "wga_sb", AT_WGA)
        nc.sync.dma_start(wga_sb[:], wga)
        wy_codes = placed([P, N], U32, "wy_codes", AT_WY)
        nc.sync.dma_start(wy_codes[:].bitcast(I32), wy_words[0].rearrange("p c i -> p (c i)").bitcast(I32))
        by_sb = placed([P, N_TILES], F32, "by_sb", AT_BY)
        with nc.allow_non_contiguous_dma(reason="one bias value for each output row"):
            nc.sync.dma_start(by_sb[:], by.rearrange("(j p) -> p j", p=P))
        wy_plane = placed([P, N], U8, "wy_plane", AT_WY_PLANE)
        nc.gpsimd.memset(wy_plane[:].bitcast(I32), 0)
        for q in range(P // QUADRANT):
            nc.sync.dma_start(wy_plane[QUADRANT * q:QUADRANT * q + PACK, :].bitcast(I32),
                              wy_scales[0, PACK * q:PACK * (q + 1), :].bitcast(I32))

        def first_stage(codes, scales, dtype, pair, h):
            acc = bank(pair)
            cols = slice(BANK * h, BANK * (h + 1))
            for a in range(PASSES):
                nc.tensor.matmul_mx(acc[:], lhsT=codes[a].bitcast(dtype), lhsT_scale=scales[a],
                                    rhs=v_codes[a][:, cols].bitcast(FP8X4), rhs_scale=planes[a][:, cols],
                                    start=(a == 0), stop=(a == PASSES - 1))
            return acc, cols

        def by_slices(raw):
            return raw[:].rearrange("p (j m t) -> p m t j", t=PACK, j=PACK)

        def as_words(rounded):
            return rounded.rearrange("p (t m j) -> p m t j", t=PACK, j=PACK)

        def mx_tiles(name):
            return kept([P, H], U32, name + "_codes"), kept([P, H], U8, name + "_plane")

        def slice_of(mx, t):
            return [codes[:, P * t:P * (t + 1)] for codes, plane in mx], [plane[:, P * t:P * (t + 1)] for codes, plane in mx]

        def quantise_pass(mx, a, rounded):
            width = PACK // (a + 1)
            for t0 in range(0, PACK, width):
                cols = slice(P * t0, P * (t0 + width))
                nc.vector.quantize_mx(mx[a][0][:, cols].bitcast(FP8X4), mx[a][1][:, cols],
                                      rounded[:, K_PASS * t0:K_PASS * (t0 + width)])

        wb_mx = [mx_tiles("wb%d" % a) for a in range(PASSES)]
        for a in range(PASSES):
            wb_rounded = kept([P, PACK * H], BF16, "wb_rounded%d" % a)
            nc.vector.tensor_copy(as_words(wb_rounded[:]), by_slices(wb_raw[a]))
            quantise_pass(wb_mx, a, wb_rounded[:])

        eb = [kept([P, S], F32, "eb%d" % t) for t in range(PACK)]
        hb = [kept([P, S], F32, "hb%d" % t) for t in range(PACK)]

        def exp_slice(t):
            codes = [we_codes[:, a, 2 * P * t:2 * P * (t + 1)] for a in range(PASSES)]
            scales = [planes[a][:, S + P * t:S + P * (t + 1)] for a in range(PASSES)]
            for h in range(HALVES):
                acc, cols = first_stage(codes, scales, FP4X4, EXP_PAIRS[t], h)
                nc.scalar.activation(eb[t][:, cols], acc[:], ACT.Exp)

        def hb_slice(t):
            codes, scales = slice_of(wb_mx, t)
            for h in range(HALVES):
                acc, cols = first_stage(codes, scales, FP8X4, HB_PAIRS[t], h)
                nc.vector.tensor_tensor(hb[t][:, cols], acc[:], eb[t][:, cols], ALU.mult)

        for step in range(PACK + EXP_LEAD):
            if step < PACK:
                exp_slice(step)
            if step >= EXP_LEAD:
                hb_slice(step - EXP_LEAD)

        wp_mx = [mx_tiles("wp%d" % a) for a in range(PASSES)]
        xb = kept([P, PACK * M], F32, "xb")
        wp_rounded = kept([P, PACK * H], BF16, "wp_rounded")
        borrowed = xb[:, 3 * M // 2:7 * M // 2].bitcast(BF16)
        for a, rounded in enumerate((wp_rounded[:], borrowed)):
            for m0 in range(0, P, P // 2):
                nc.scalar.copy(as_words(rounded)[:, m0:m0 + P // 2], by_slices(wp_raw[a])[:, m0:m0 + P // 2])
            quantise_pass(wp_mx, a, rounded)
        hp = [kept([P, S], F32, "hp%d" % t) for t in range(PACK)]
        for t in range(PACK):
            codes, scales = slice_of(wp_mx, t)
            for h in range(HALVES):
                acc, cols = first_stage(codes, scales, FP8X4, HP_PAIRS[t], h)
                nc.scalar.activation(hp[t][:, cols], acc[:], ACT.Identity, bias=bp_sb[:, t:t + 1])

        def pick(picked, h_slices, offsets, weights, m0, width):
            entries = offsets[:, m0 // LIST_ROWS:(m0 + width) // LIST_ROWS]
            for t in range(PACK):
                nc.vector.tensor_tensor(picked[:, t, :], h_slices[t][:].indirect(entries),
                                        weights[:, m0:m0 + width], ALU.mult)

        xb_slices = xb[:].rearrange("p (t m) -> p t m", t=PACK)
        pick(xb_slices, hb, offs3_sb, wgb_sb, 0, M)

        out_rows = out.rearrange("(j p) m -> p j m", p=P)
        for piece, (m0, width) in enumerate(PIECES):
            xa = placed([P, PACK, width], F32, "xa%d" % piece, AT_XA)
            pick(xa, hp, offs2_sb, wga_sb, m0, width)
            z = kept([P, PACK * width], BF16, "z%d" % piece)
            nc.vector.tensor_tensor(z[:].rearrange("p (c i t) -> p c t i", i=2, t=PACK),
                                    xa[:].rearrange("p t (c i) -> p c t i", i=2),
                                    xb_slices[:, :, m0:m0 + width].rearrange("p t (c i) -> p c t i", i=2), ALU.max)
            z_codes = kept([P, width], U32, "z_codes%d" % piece)
            z_plane = kept([P, width], U8, "z_plane%d" % piece)
            nc.vector.quantize_mx(z_codes[:].bitcast(FP8X4), z_plane[:], z[:])
            scores = kept([P, N_TILES, width], F32, "scores%d" % piece)
            for j in range(N_TILES):
                acc = bank(j % PAIRS)
                for c0 in range(0, width, MAX_MOVING):
                    cols = slice(c0, min(c0 + MAX_MOVING, width))
                    nc.tensor.matmul_mx(acc[:, cols], lhsT=wy_codes[:, P * j:P * (j + 1)].bitcast(FP8X4),
                                        lhsT_scale=wy_plane[:, P * j:P * (j + 1)],
                                        rhs=z_codes[:, cols].bitcast(FP8X4), rhs_scale=z_plane[:, cols],
                                        start=True, stop=True)
                nc.scalar.activation(scores[:, j, :], acc[:, 0:width], ACT.Tanh, bias=by_sb[:, j:j + 1])
                if j % STORE_TILES == STORE_TILES - 1:
                    rows = slice(j + 1 - STORE_TILES, j + 1)
                    nc.sync.dma_start(out_rows[:, rows, m0:m0 + width], scores[:, rows, :])
